import numpy as np
import ml_dtypes


def mxq(x, axis, fmt="e4m3"):
    dtype, down = {"e4m3": (ml_dtypes.float8_e4m3fn, 7), "e5m2": (ml_dtypes.float8_e5m2, 14)}[fmt]
    v = np.moveaxis(np.asarray(x, np.float32).astype(ml_dtypes.bfloat16).astype(np.float64), axis, -1)
    blocks = v.reshape(v.shape[:-1] + (-1, 32))
    amax = np.abs(blocks).max(-1, keepdims=True)
    byte = np.maximum(np.where(amax > 0, np.frexp(amax)[1] - 1 + 127, 0) - down, 1)
    scale = np.exp2(byte - 127.0)
    codes = (blocks / scale).astype(np.float32).astype(dtype).astype(np.float64)
    return np.moveaxis((codes * scale).reshape(v.shape), -1, axis)


WIDE = False


def mx_kscale(k):
    if not WIDE:
        return np.ones(k)
    levels = np.array([10, -10, 5, -5, 0])
    if k % 512:
        return np.exp2(np.random.permutation(np.resize(levels, k // 32))).repeat(32)
    a = np.empty((k // 512, 16))
    for p in range(k // 512):
        a[p, :8] = np.random.permutation(np.resize(levels, 8))
        for g in range(8):
            far = levels[np.abs(levels - a[p, g]) >= 10]
            a[p, g + 8] = far[np.random.randint(len(far))]
    return np.exp2(a.ravel()).repeat(32)


def f64(x):
    return np.asarray(x).astype(np.float64)


def striped(idx):
    return np.tile(idx.reshape(-1, 16).T, (8, 1)).astype(np.uint16)


def unstriped(offs):
    return offs[:16].T.reshape(-1).astype(np.int64)


def striped8(idx):
    return np.concatenate([x.reshape(-1, 16).T for x in idx]).astype(np.uint16)


def runs(offs, k):
    lists = np.stack([offs[16 * r : 16 * r + 16].T.reshape(-1) for r in range(8)]).astype(np.int64)
    return lists[np.arange(k) % 512 // 64]


def pack_weight(w):
    k, n = w.shape
    w = f64(np.asarray(w, np.float32).astype(ml_dtypes.bfloat16)).reshape(k // 32, 32, n)
    amax = np.abs(w).max(1)
    byte = np.clip(np.where(amax > 0, np.frexp(amax)[1] - 1 + 127 - 7, 1), 1, 254)
    scaled = (w * np.exp2(127.0 - byte)[:, None, :]).reshape(k, n).astype(np.float32)
    words = np.ascontiguousarray(scaled.reshape(k // 512, 128, 4, n).transpose(0, 1, 3, 2)).astype(ml_dtypes.float8_e4m3fn).view(np.uint8)
    return words, np.ascontiguousarray(byte.astype(np.uint8).reshape(k // 512, 16, n))


def unpack_weight(words, scales):
    g, p, n, _ = words.shape
    vals = np.ascontiguousarray(words).view(ml_dtypes.float8_e4m3fn).astype(np.float64) * np.repeat(np.exp2(scales.astype(np.float64) - 127.0), 8, axis=1)[..., None]
    return vals.transpose(0, 1, 3, 2).reshape(g * 512, n)


E2M1 = np.array([0.0, 0.5, 1.0, 1.5, 2.0, 3.0, 4.0, 6.0, -0.0, -0.5, -1.0, -1.5, -2.0, -3.0, -4.0, -6.0])


def pack_fp4(w):
    k, n = w.shape
    w = f64(np.asarray(w, np.float32).astype(ml_dtypes.bfloat16)).reshape(k // 32, 32, n)
    amax = np.abs(w).max(1)
    mant, ex = np.frexp(amax / 6.0)
    byte = np.clip(np.where(amax > 0, np.where(mant > 0.5, ex, ex - 1) + 127, 1), 1, 254)
    scaled = (w * np.exp2(127.0 - byte)[:, None, :]).reshape(k, n).astype(np.float32)
    c = np.ascontiguousarray(scaled.reshape(k // 512, 128, 4, n).transpose(0, 1, 3, 2)).astype(ml_dtypes.float4_e2m1fn).view(np.uint8) & 0xF
    words = (c[..., 0::2] | (c[..., 1::2] << 4)).reshape(k // 512, 128, 2 * n)
    return np.ascontiguousarray(words), np.ascontiguousarray(byte.astype(np.uint8).reshape(k // 512, 16, n))


def unpack_fp4(words, scales):
    g, _, n = scales.shape
    words = np.ascontiguousarray(words).reshape(g, 128, n, 2)
    nib = np.empty((g, 128, n, 4), np.uint8)
    nib[..., 0::2] = words & 0xF
    nib[..., 1::2] = words >> 4
    vals = E2M1[nib] * np.repeat(np.exp2(scales.astype(np.float64) - 127.0), 8, axis=1)[..., None]
    return vals.transpose(0, 1, 3, 2).reshape(g * 512, n)


def sigmoid(v):
    return 1.0 / (1.0 + np.exp(-np.maximum(v, -700.0)))

def planes(y):
    n, m = y.shape
    v = y.astype(np.float32).astype(ml_dtypes.bfloat16).astype(np.float64).reshape(n // 32, 32, m)
    top = np.abs(v).max(1)
    byte = np.clip(np.where(top > 0, np.frexp(top)[1] - 1 + 127 - 7, 1), 1, 254)
    codes = (v * np.exp2(127.0 - byte)[:, None, :]).reshape(n, m).astype(np.float32).astype(ml_dtypes.float8_e4m3fn).view(np.uint8)
    words = codes.reshape(n // 512, 128, 4, m).transpose(0, 1, 3, 2)
    return np.ascontiguousarray(words), np.ascontiguousarray(byte.astype(np.uint8).reshape(n // 512, 16, m))


K, T, S, N, H = 512, 2048, 512, 512, 512


def setup_inputs():
    n = np.random.standard_normal
    s = mx_kscale(K)[:, None]
    u = mx_kscale(H)
    packed_xT = pack_weight(n((K, T)) * s)
    packed_w1 = pack_fp4(n((K, H)) / np.sqrt(K) / s)
    packed_w2 = pack_fp4(n((H, N)) / np.sqrt(H) / u[:, None])
    return {
        "x_words": packed_xT[0],
        "x_scales": packed_xT[1],
        "w1_words": packed_w1[0],
        "w1_scales": packed_w1[1],
        "gn": (np.random.uniform(0.5, 1.5, (H, 1)) * u[:, None]).astype(np.float32),
        "w2_words": packed_w2[0],
        "w2_scales": packed_w2[1],
        "offs": striped(np.random.permutation(T)[:S]),
        "n1": striped8(np.stack([np.random.permutation(S) for _ in range(8)])),
        "n2": striped8(np.stack([np.random.permutation(S) for _ in range(8)])),
        "n3": striped8(np.stack([np.random.permutation(S) for _ in range(8)])),
        "n4": striped8(np.stack([np.random.permutation(S) for _ in range(8)])),
    }


def reference(x_words, x_scales, w1_words, w1_scales, gn, w2_words, w2_scales, offs, n1, n2, n3, n4):
    xq = unpack_weight(x_words, x_scales)[:, unstriped(offs)]
    y = unpack_fp4(w1_words, w1_scales).T @ xq
    pa = y[np.arange(H)[:, None], runs(n1, H)]
    pb = y[np.arange(H)[:, None], runs(n2, H)]
    z = f64(gn) * (np.maximum(np.minimum(y, pa), np.minimum(np.maximum(y, pa), pb)))
    h = unpack_fp4(w2_words, w2_scales).T @ mxq(z, 0, "e4m3")
    sm = np.maximum(h, h[np.arange(N)[:, None], runs(n4, N)])
    ds = np.zeros((N, S))
    ds[np.arange(N)[:, None], runs(n3, N)] = sm
    out_0 = ds * sigmoid(h)
    return (out_0,) + planes(out_0)

@@ -1,0 +1,309 @@
+from contextlib import ExitStack
+
+import concourse.mybir as mybir
+
+F32 = mybir.dt.float32
+BF16 = mybir.dt.bfloat16
+I32 = mybir.dt.int32
+U32 = mybir.dt.uint32
+U16 = mybir.dt.uint16
+U8 = mybir.dt.uint8
+FP8X4 = mybir.dt.float8_e4m3fn_x4
+FP4X4 = mybir.dt.float4_e2m1fn_x4
+ALU = mybir.AluOpType
+ACT = mybir.ActivationFunctionType
+
+P = 128
+PACK = 4
+TOKENS = 2048
+S = 512
+HALF = S // 2
+CHUNKS = ((0, 256), (256, 128), (384, 128))
+FLOPS = 2 * 2 * 512 * 512 * 512
+
+
+def tile_picked_laymedsendg_none_po_kernel(
+    tc, x_words, x_scales, w1_words, w1_scales, gn, w2_words, w2_scales, offs, n1, n2, n3, n4, out_0, out_1, out_2
+):
+    nc = tc.nc
+    with ExitStack() as ctx:
+        keep = ctx.enter_context(tc.tile_pool(name="keep", bufs=1))
+        psum = ctx.enter_context(tc.psum_pool(name="psum", bufs=1))
+
+        def load_scale_rows(queue, tile, rows, quadrants):
+            for q in quadrants:
+                queue.dma_start(out=tile[32 * q : 32 * q + 4, :].bitcast(I32), in_=rows[0, 4 * q : 4 * q + 4, :].bitcast(I32))
+
+        def load_list(name, src):
+            tile = keep.tile([P, S // 16], U16, name=name)
+            nc.sync.dma_start(tile[:], src)
+            return tile
+
+        def entries(lst, start, count):
+            return lst[:, start // 16 : (start + count) // 16]
+
+        def deal_words(name, raw):
+            dealt = keep.tile([P, 2 * S], U8, name=name, align_bytes=64)
+            nc.vector.tensor_copy(
+                out=dealt[:].rearrange("p (t m e) -> p t m e", t=PACK, e=2),
+                in_=raw[:].rearrange("p (m t e) -> p t m e", t=PACK, e=2),
+            )
+            return dealt
+
+        def deal_scales(name, raw):
+            dealt = keep.tile([P, S], U8, name=name, align_bytes=64)
+            nc.vector.tensor_copy(
+                out=dealt[:].rearrange("p (t m) -> p t m", t=PACK),
+                in_=raw[:].rearrange("p (m t) -> p t m", t=PACK),
+            )
+            return dealt
+
+        w1s_raw = keep.tile([P, S], U8, name="w1s_raw")
+        xs_all = keep.tile([P, TOKENS], U8, name="xs_all")
+        w2s_raw = keep.tile([P, S], U8, name="w2s_raw")
+        nc.gpsimd.memset(w1s_raw[:].bitcast(I32), 0)
+        nc.vector.memset(xs_all[:].bitcast(I32), 0)
+        nc.vector.memset(w2s_raw[:].bitcast(I32), 0)
+
+        w1w_raw = keep.tile([P, 2 * S], U8, name="w1w_raw")
+        w2w_raw = keep.tile([P, 2 * S], U8, name="w2w_raw")
+        xw_all = keep.tile([P, TOKENS], U32, name="xw_all")
+        gain = keep.tile([P, PACK], F32, name="gain")
+
+        offs_t = load_list("offs_t", offs)
+        nc.sync.dma_start(out=w1w_raw[:].bitcast(I32), in_=w1_words[0].bitcast(I32))
+        nc.sync.dma_start(out=xw_all[:].bitcast(I32), in_=x_words[0].rearrange("p c r -> p (c r)").bitcast(I32))
+        load_scale_rows(nc.scalar, xs_all, x_scales, range(4))
+        load_scale_rows(nc.scalar, w1s_raw, w1_scales, range(2))
+        load_scale_rows(nc.gpsimd, w1s_raw, w1_scales, range(2, 4))
+        nc.sync.dma_start(out=gain[:], in_=gn.rearrange("(p t) o -> p (t o)", t=PACK))
+        n1_t = load_list("n1_t", n1)
+        n2_t = load_list("n2_t", n2)
+        nc.sync.dma_start(out=w2w_raw[:].bitcast(I32), in_=w2_words[0].bitcast(I32))
+        load_scale_rows(nc.sync, w2s_raw, w2_scales, range(4))
+        n4_t = load_list("n4_t", n4)
+        n3_t = load_list("n3_t", n3)
+
+        w1w = deal_words("w1w", w1w_raw)
+        w1s = deal_scales("w1s", w1s_raw)
+
+        xs = keep.tile([P, S], U8, name="xs", align_bytes=64)
+        nc.vector.tensor_copy(xs[:], xs_all[:].indirect(offs_t[:]))
+
+        y_win = [keep.tile([P, S], F32, name=f"y_win{t}") for t in range(PACK)]
+        y_own = keep.tile([P, PACK, S], F32, name="y_own")
+        y_ps = {}
+        xw = []
+        for half in range(2):
+            xw.append(keep.tile([P, HALF], U32, name=f"xw{half}", align_bytes=64))
+            nc.vector.tensor_copy(xw[half][:], xw_all[:].indirect(entries(offs_t, half * HALF, HALF)))
+        y_banks = [psum.tile([P, 2, HALF], F32, name=f"y_ps{b}") for b in range(4)]
+
+        def first_product(half, t):
+            y_ps[half, t] = y_banks[2 * (t % 2) + half][:, t // 2, :]
+            nc.tensor.matmul_mx(
+                out=y_ps[half, t],
+                lhsT=w1w[:, 2 * P * t : 2 * P * (t + 1)].bitcast(FP4X4),
+                lhsT_scale=w1s[:, P * t : P * (t + 1)],
+                rhs=xw[half][:].bitcast(FP8X4),
+                rhs_scale=xs[:, half * HALF : (half + 1) * HALF],
+                start=True,
+                stop=True,
+            )
+
+        def y_out(dst, half, t):
+            nc.scalar.activation(out=dst, in_=y_ps[half, t], func=ACT.Copy, scale=gain[:, t : t + 1])
+
+        for t in range(PACK):
+            first_product(0, t)
+            first_product(1, t)
+            y_out(y_win[t][:, :HALF], 0, t)
+            y_out(y_own[:, t, :HALF], 0, t)
+            y_out(y_win[t][:, HALF:], 1, t)
+        for t in range(PACK):
+            y_out(y_own[:, t, HALF:], 1, t)
+
+        w2w = deal_words("w2w", w2w_raw)
+        w2s = deal_scales("w2s", w2s_raw)
+
+        h_win = [keep.tile([P, S], F32, name=f"h_win{t}") for t in range(PACK)]
+        h_own = keep.tile([P, PACK, S], F32, name="h_own")
+        gate = keep.tile([P, PACK, S], F32, name="gate")
+
+        da, db, mid, med, z32 = {}, {}, {}, {}, {}
+
+        def gathers(c):
+            start, n = CHUNKS[c]
+            da[c] = keep.tile([P, PACK, n], F32, name=f"da{c}")
+            db[c] = keep.tile([P, PACK, n], F32, name=f"db{c}", tag="z16_0" if c == 2 else f"db{c}", align_bytes=64)
+            steps = []
+            for t in range(PACK):
+                for dst, lst in ((da[c], n1_t), (db[c], n2_t)):
+                    steps.append((dst[:, t, :], y_win[t][:].indirect(entries(lst, start, n)), y_own[:, t, start : start + n]))
+            return steps
+
+        def run(steps):
+            for dst, looked, own in steps:
+                nc.vector.tensor_tensor(dst, looked, own, ALU.subtract)
+
+        def upper(c, ts):
+            nc.vector.scalar_tensor_tensor(out=mid[c][:, ts, :], in0=da[c][:, ts, :], scalar=0.0, in1=db[c][:, ts, :], op0=ALU.max, op1=ALU.min)
+
+        def lower(c, ts):
+            nc.vector.scalar_tensor_tensor(out=med[c][:, ts, :], in0=da[c][:, ts, :], scalar=0.0, in1=mid[c][:, ts, :], op0=ALU.min, op1=ALU.max)
+
+        def add_back(c, ts):
+            start, n = CHUNKS[c]
+            nc.vector.tensor_tensor(z32[c][:, ts, :], med[c][:, ts, :], y_own[:, ts, start : start + n], ALU.add)
+
+        def alloc(c):
+            n = CHUNKS[c][1]
+            mid[c] = keep.tile([P, PACK, n], F32, name=f"mid{c}", tag="z16_1" if c == 2 else f"mid{c}", align_bytes=64)
+            med[c] = keep.tile([P, PACK, n], F32, name=f"med{c}")
+            z32[c] = keep.tile([P, PACK, n], F32, name=f"z32{c}")
+
+        z16 = {}
+
+        def weave(c, last):
+            n = CHUNKS[c][1]
+            z16[c] = keep.tile([P, n, PACK], BF16, name=f"z16{c}", tag=f"z16_{c}", align_bytes=64)
+            src = z32[c][:].rearrange("p t c -> p c t")
+            if last:
+                nc.vector.tensor_copy(out=z16[c][:], in_=src)
+            else:
+                nc.scalar.copy(out=z16[c][:], in_=src)
+
+        def second_product(c):
+            start, n = CHUNKS[c]
+            cols = slice(start, start + n)
+            zw = keep.tile([P, n], U32, name=f"zw{c}", align_bytes=64)
+            zs = keep.tile([P, n], U8, name=f"zs{c}", align_bytes=64)
+            nc.vector.quantize_mx(out=zw[:].bitcast(FP8X4), scales=zs[:], in_=z16[c][:].rearrange("p c t -> p (c t)"))
+            per_bank = S // n
+            banks = []
+            for t0 in range(0, PACK, per_bank):
+                bank = psum.tile([P, per_bank, n], F32, name=f"h_ps{c}{t0}")
+                banks.append((t0, bank))
+                for e in range(per_bank):
+                    t = t0 + e
+                    nc.tensor.matmul_mx(
+                        out=bank[:, e, :],
+                        lhsT=w2w[:, 2 * P * t : 2 * P * (t + 1)].bitcast(FP4X4),
+                        lhsT_scale=w2s[:, P * t : P * (t + 1)],
+                        rhs=zw[:].bitcast(FP8X4),
+                        rhs_scale=zs[:],
+                        start=True,
+                        stop=True,
+                    )
+            return banks
+
+        def h_window(c, banks, t):
+            start, n = CHUNKS[c]
+            per_bank = S // n
+            nc.scalar.copy(out=h_win[t][:, start : start + n], in_=banks[t // per_bank][1][:, t % per_bank, :])
+
+        def h_plain(c, banks):
+            start, n = CHUNKS[c]
+            for t0, bank in banks:
+                nc.scalar.copy(out=h_own[:, t0 : t0 + S // n, start : start + n], in_=bank[:])
+
+        def gates(t):
+            nc.scalar.activation(out=gate[:, t, :], in_=h_own[:, t, :], func=ACT.Sigmoid)
+
+        every = slice(0, PACK)
+        alloc(0)
+        alloc(1)
+        run(gathers(0))
+        nxt = gathers(1)
+        upper(0, every)
+        run(nxt[:2])
+        lower(0, every)
+        run(nxt[2:4])
+        add_back(0, every)
+        weave(0, False)
+        run(nxt[4:])
+        banks0 = second_product(0)
+        nxt = gathers(2)
+        upper(1, every)
+        run(nxt[0:4:2])
+        lower(1, every)
+        run(nxt[4::2])
+        add_back(1, every)
+        weave(1, False)
+        for t in range(PACK):
+            h_window(0, banks0, t)
+        h_plain(0, banks0)
+        run(nxt[1::2])
+        banks1 = second_product(1)
+        alloc(2)
+        lo, hi = slice(0, 2), slice(2, 4)
+        upper(2, lo)
+        upper(2, hi)
+        lower(2, lo)
+        lower(2, hi)
+        add_back(2, lo)
+        add_back(2, hi)
+        weave(2, True)
+        banks2 = second_product(2)
+        h_window(1, banks1, 0)
+        h_window(2, banks2, 0)
+        h_plain(1, banks1)
+        h_plain(2, banks2)
+        for t in range(1, PACK):
+            h_window(1, banks1, t)
+            h_window(2, banks2, t)
+
+        out_rows = out_0.rearrange("(p t) c -> p t c", t=PACK)
+        res = keep.tile([P, PACK, S], F32, name="res")
+        rise = {}
+        sent = {}
+
+        def look_up(t):
+            diff = keep.tile([P, S], F32, name=f"diff{t}")
+            for half in range(2):
+                cols = slice(half * HALF, (half + 1) * HALF)
+                nc.vector.tensor_tensor(diff[:, cols], h_win[t][:].indirect(entries(n4_t, half * HALF, HALF)), h_own[:, t, cols], ALU.subtract)
+            rise[t] = keep.tile([P, S], F32, name=f"rise{t}")
+            nc.scalar.activation(out=rise[t][:], in_=diff[:], func=ACT.Relu)
+
+        def send(t):
+            sent[t] = keep.tile([P, 2 * S], F32, name=f"sent{t}")
+            nc.vector.tensor_tensor(sent[t][:].indirect(n3_t[:]), h_own[:, t, :], rise[t][:], ALU.add)
+
+        def finish(t, cols):
+            nc.vector.tensor_tensor(res[:, t, cols], sent[t][:, cols], gate[:, t, cols], ALU.mult)
+            nc.sync.dma_start(out=out_rows[:, t, cols], in_=res[:, t, cols])
+
+        whole = slice(0, S)
+        look_up(0)
+        look_up(1)
+        gates(0)
+        send(0)
+        look_up(2)
+        gates(1)
+        send(1)
+        finish(0, whole)
+        look_up(3)
+        gates(2)
+        gates(3)
+        send(2)
+        finish(1, whole)
+        finish(2, whole)
+        send(3)
+
+        ow = keep.tile([P, S], U32, name="ow", align_bytes=64)
+        osc = keep.tile([P, S], U8, name="osc", align_bytes=64)
+        words_out = out_1[0].rearrange("p c r -> p (c r)").bitcast(I32)
+        o16 = [keep.tile([P, HALF, PACK], BF16, name=f"o16{half}", align_bytes=64) for half in range(2)]
+        halves = [slice(half * HALF, (half + 1) * HALF) for half in range(2)]
+        finish(3, halves[0])
+        nc.scalar.copy(out=o16[0][:], in_=res[:, :, halves[0]].rearrange("p t c -> p c t"))
+        finish(3, halves[1])
+        nc.vector.tensor_copy(out=o16[1][:], in_=res[:, :, halves[1]].rearrange("p t c -> p c t"))
+        for half in (1, 0):
+            cols = halves[half]
+            nc.vector.quantize_mx(out=ow[:, cols].bitcast(FP8X4), scales=osc[:, cols], in_=o16[half][:].rearrange("p c t -> p (c t)"))
+            nc.sync.dma_start(out=words_out[:, cols], in_=ow[:, cols].bitcast(I32))
+        for q in range(4):
+            queue = nc.scalar if q % 2 else nc.sync
+            queue.dma_start(out=out_2[0, 4 * q : 4 * q + 4, :].bitcast(I32), in_=osc[32 * q : 32 * q + 4, :].bitcast(I32))

@@ -1,6 +1,7 @@
 from contextlib import ExitStack
 
 import concourse.mybir as mybir
+from concourse.masks import make_identity
 
 F32 = mybir.dt.float32
 BF16 = mybir.dt.bfloat16
@@ -19,6 +20,11 @@ TOKENS = 2048
 S = 512
 HALF = S // 2
 CHUNKS = ((0, 256), (256, 128), (384, 128))
+H_BANKS = (
+    ((0, 2, "h0"), (2, 4, "h1")),
+    ((0, 4, "h2"),),
+    ((0, 1, "h3"), (1, 4, "shared1")),
+)
 FLOPS = 2 * 2 * 512 * 512 * 512
 
 
@@ -42,8 +48,8 @@ def tile_picked_laymedsendg_none_po_kernel(
         def entries(lst, start, count):
             return lst[:, start // 16 : (start + count) // 16]
 
-        def deal_words(name, raw):
-            dealt = keep.tile([P, 2 * S], U8, name=name, align_bytes=64)
+        def deal_words(name, raw, tag):
+            dealt = keep.tile([P, 2 * S], U8, name=name, tag=tag, align_bytes=64)
             nc.vector.tensor_copy(
                 out=dealt[:].rearrange("p (t m e) -> p t m e", t=PACK, e=2),
                 in_=raw[:].rearrange("p (m t e) -> p t m e", t=PACK, e=2),
@@ -61,30 +67,32 @@ def tile_picked_laymedsendg_none_po_kernel(
         w1s_raw = keep.tile([P, S], U8, name="w1s_raw")
         xs_all = keep.tile([P, TOKENS], U8, name="xs_all")
         w2s_raw = keep.tile([P, S], U8, name="w2s_raw")
-        nc.gpsimd.memset(w1s_raw[:].bitcast(I32), 0)
-        nc.vector.memset(xs_all[:].bitcast(I32), 0)
+        nc.gpsimd.memset(xs_all[:].bitcast(I32), 0)
+        nc.vector.memset(w1s_raw[:].bitcast(I32), 0)
         nc.vector.memset(w2s_raw[:].bitcast(I32), 0)
 
         w1w_raw = keep.tile([P, 2 * S], U8, name="w1w_raw")
         w2w_raw = keep.tile([P, 2 * S], U8, name="w2w_raw")
-        xw_all = keep.tile([P, TOKENS], U32, name="xw_all")
+        xw_all = keep.tile([P, TOKENS], U32, name="xw_all", tag="xw_all", align_bytes=64)
         gain = keep.tile([P, PACK], F32, name="gain")
 
         offs_t = load_list("offs_t", offs)
         nc.sync.dma_start(out=w1w_raw[:].bitcast(I32), in_=w1_words[0].bitcast(I32))
         nc.sync.dma_start(out=xw_all[:].bitcast(I32), in_=x_words[0].rearrange("p c r -> p (c r)").bitcast(I32))
         load_scale_rows(nc.scalar, xs_all, x_scales, range(4))
-        load_scale_rows(nc.scalar, w1s_raw, w1_scales, range(2))
-        load_scale_rows(nc.gpsimd, w1s_raw, w1_scales, range(2, 4))
-        nc.sync.dma_start(out=gain[:], in_=gn.rearrange("(p t) o -> p (t o)", t=PACK))
+        load_scale_rows(nc.scalar, w1s_raw, w1_scales, range(3))
+        nc.gpsimd.dma_start(out=gain[:], in_=gn.rearrange("(p t) o -> p (t o)", t=PACK))
+        load_scale_rows(nc.gpsimd, w1s_raw, w1_scales, range(3, 4))
+        nc.gpsimd.dma_start(out=w2w_raw[:].bitcast(I32), in_=w2_words[0].bitcast(I32))
         n1_t = load_list("n1_t", n1)
         n2_t = load_list("n2_t", n2)
-        nc.sync.dma_start(out=w2w_raw[:].bitcast(I32), in_=w2_words[0].bitcast(I32))
         load_scale_rows(nc.sync, w2s_raw, w2_scales, range(4))
         n4_t = load_list("n4_t", n4)
         n3_t = load_list("n3_t", n3)
+        ident = keep.tile([P, P], F32, name="ident")
+        make_identity(nc, ident[:])
 
-        w1w = deal_words("w1w", w1w_raw)
+        w1w = deal_words("w1w", w1w_raw, "w1w")
         w1s = deal_scales("w1s", w1s_raw)
 
         xs = keep.tile([P, S], U8, name="xs", align_bytes=64)
@@ -97,7 +105,7 @@ def tile_picked_laymedsendg_none_po_kernel(
         for half in range(2):
             xw.append(keep.tile([P, HALF], U32, name=f"xw{half}", align_bytes=64))
             nc.vector.tensor_copy(xw[half][:], xw_all[:].indirect(entries(offs_t, half * HALF, HALF)))
-        y_banks = [psum.tile([P, 2, HALF], F32, name=f"y_ps{b}") for b in range(4)]
+        y_banks = [psum.tile([P, 2, HALF], F32, name=f"y_ps{b}", tag=f"shared{b}") for b in range(4)]
 
         def first_product(half, t):
             y_ps[half, t] = y_banks[2 * (t % 2) + half][:, t // 2, :]
@@ -123,7 +131,7 @@ def tile_picked_laymedsendg_none_po_kernel(
         for t in range(PACK):
             y_out(y_own[:, t, HALF:], 1, t)
 
-        w2w = deal_words("w2w", w2w_raw)
+        w2w = deal_words("w2w", w2w_raw, "xw_all")
         w2s = deal_scales("w2s", w2s_raw)
 
         h_win = [keep.tile([P, S], F32, name=f"h_win{t}") for t in range(PACK)]
@@ -146,32 +154,46 @@ def tile_picked_laymedsendg_none_po_kernel(
             for dst, looked, own in steps:
                 nc.vector.tensor_tensor(dst, looked, own, ALU.subtract)
 
-        def upper(c, ts):
-            nc.vector.scalar_tensor_tensor(out=mid[c][:, ts, :], in0=da[c][:, ts, :], scalar=0.0, in1=db[c][:, ts, :], op0=ALU.max, op1=ALU.min)
+        def upper(c, cols):
+            nc.vector.scalar_tensor_tensor(out=mid[c][:, :, cols], in0=da[c][:, :, cols], scalar=0.0, in1=db[c][:, :, cols], op0=ALU.max, op1=ALU.min)
 
-        def lower(c, ts):
-            nc.vector.scalar_tensor_tensor(out=med[c][:, ts, :], in0=da[c][:, ts, :], scalar=0.0, in1=mid[c][:, ts, :], op0=ALU.min, op1=ALU.max)
+        def lower(c, cols):
+            nc.vector.scalar_tensor_tensor(out=med[c][:, :, cols], in0=da[c][:, :, cols], scalar=0.0, in1=mid[c][:, :, cols], op0=ALU.min, op1=ALU.max)
 
-        def add_back(c, ts):
-            start, n = CHUNKS[c]
-            nc.vector.tensor_tensor(z32[c][:, ts, :], med[c][:, ts, :], y_own[:, ts, start : start + n], ALU.add)
+        def add_back(c, cols):
+            start = CHUNKS[c][0]
+            nc.vector.tensor_tensor(z32[c][:, :, cols], med[c][:, :, cols], y_own[:, :, start + cols.start : start + cols.stop], ALU.add)
 
         def alloc(c):
             n = CHUNKS[c][1]
-            mid[c] = keep.tile([P, PACK, n], F32, name=f"mid{c}", tag="z16_1" if c == 2 else f"mid{c}", align_bytes=64)
+            mid[c] = keep.tile([P, PACK, n], F32, name=f"mid{c}", align_bytes=64)
             med[c] = keep.tile([P, PACK, n], F32, name=f"med{c}")
-            z32[c] = keep.tile([P, PACK, n], F32, name=f"z32{c}")
 
         z16 = {}
+        h_ps = {}
+        h_banks = [[], [], []]
 
-        def weave(c, last):
-            n = CHUNKS[c][1]
-            z16[c] = keep.tile([P, n, PACK], BF16, name=f"z16{c}", tag=f"z16_{c}", align_bytes=64)
-            src = z32[c][:].rearrange("p t c -> p c t")
-            if last:
-                nc.vector.tensor_copy(out=z16[c][:], in_=src)
-            else:
-                nc.scalar.copy(out=z16[c][:], in_=src)
+        def z_tile(c):
+            z16[c] = keep.tile([P, CHUNKS[c][1], PACK], BF16, name=f"z16{c}", tag=f"z16_{c}", align_bytes=64)
+
+        def weave(c, cols):
+            nc.vector.tensor_copy(out=z16[c][:, cols, :], in_=z32[c][:, :, cols].rearrange("p t c -> p c t"))
+
+        def add_turned(c, off):
+            start = CHUNKS[c][0] + off
+            blk = start // P
+            turned = psum.tile([P, PACK, P], F32, name=f"turned{blk}", tag=f"shared{blk % 2}")
+            for t in range(PACK):
+                nc.tensor.matmul(turned[:, t, :], lhsT=y_own[:, t, start : start + P], rhs=ident[:], start=True, stop=False, is_transpose=True)
+                nc.tensor.matmul(turned[:, t, :], lhsT=med[c][:, t, off : off + P], rhs=ident[:], start=False, stop=True, is_transpose=True)
+            pairs = keep.tile([P, 2, P, 2], BF16, name=f"pairs{blk}")
+            nc.scalar.copy(out=pairs[:], in_=turned[:].rearrange("j (u e) p -> j u p e", e=2))
+            words = pairs[:].rearrange("j u p e -> j (u p e)").bitcast(F32)
+            back = psum.tile([P, 2, P], F32, name=f"back{blk}", tag=f"shared{2 + blk % 2}")
+            for u in range(2):
+                nc.tensor.transpose(back[:, u, :], words[:, u * P : (u + 1) * P], ident[:])
+            dst = z16[c][:, off : off + P, :].rearrange("p c t -> p (c t)").bitcast(F32)
+            nc.scalar.copy(out=dst.rearrange("p (j u) -> p j u", u=2), in_=back[:].rearrange("p u j -> p j u"))
 
         def second_product(c):
             start, n = CHUNKS[c]
@@ -179,15 +201,13 @@ def tile_picked_laymedsendg_none_po_kernel(
             zw = keep.tile([P, n], U32, name=f"zw{c}", align_bytes=64)
             zs = keep.tile([P, n], U8, name=f"zs{c}", align_bytes=64)
             nc.vector.quantize_mx(out=zw[:].bitcast(FP8X4), scales=zs[:], in_=z16[c][:].rearrange("p c t -> p (c t)"))
-            per_bank = S // n
-            banks = []
-            for t0 in range(0, PACK, per_bank):
-                bank = psum.tile([P, per_bank, n], F32, name=f"h_ps{c}{t0}")
-                banks.append((t0, bank))
-                for e in range(per_bank):
-                    t = t0 + e
+            for first, last, tag in H_BANKS[c]:
+                bank = psum.tile([P, last - first, n], F32, name=f"h_ps{c}{first}", tag=tag)
+                h_banks[c].append((first, last, bank))
+                for t in range(first, last):
+                    h_ps[c, t] = bank[:, t - first, :]
                     nc.tensor.matmul_mx(
-                        out=bank[:, e, :],
+                        out=h_ps[c, t],
                         lhsT=w2w[:, 2 * P * t : 2 * P * (t + 1)].bitcast(FP4X4),
                         lhsT_scale=w2s[:, P * t : P * (t + 1)],
                         rhs=zw[:].bitcast(FP8X4),
@@ -195,63 +215,61 @@ def tile_picked_laymedsendg_none_po_kernel(
                         start=True,
                         stop=True,
                     )
-            return banks
 
-        def h_window(c, banks, t):
-            start, n = CHUNKS[c]
-            per_bank = S // n
-            nc.scalar.copy(out=h_win[t][:, start : start + n], in_=banks[t // per_bank][1][:, t % per_bank, :])
+        def h_window(t):
+            for c, (start, n) in enumerate(CHUNKS):
+                nc.scalar.copy(out=h_win[t][:, start : start + n], in_=h_ps[c, t])
 
-        def h_plain(c, banks):
-            start, n = CHUNKS[c]
-            for t0, bank in banks:
-                nc.scalar.copy(out=h_own[:, t0 : t0 + S // n, start : start + n], in_=bank[:])
+        def h_plain(first, last):
+            for c, (start, n) in enumerate(CHUNKS):
+                for b_first, b_last, bank in h_banks[c]:
+                    lo_t, hi_t = max(first, b_first), min(last, b_last)
+                    if lo_t < hi_t:
+                        nc.scalar.copy(out=h_own[:, lo_t:hi_t, start : start + n], in_=bank[:, lo_t - b_first : hi_t - b_first, :])
 
         def gates(t):
             nc.scalar.activation(out=gate[:, t, :], in_=h_own[:, t, :], func=ACT.Sigmoid)
 
-        every = slice(0, PACK)
-        alloc(0)
-        alloc(1)
+        every, lo, hi = slice(0, HALF), slice(0, P // 2), slice(P // 2, P)
+        for c in range(3):
+            alloc(c)
         run(gathers(0))
         nxt = gathers(1)
         upper(0, every)
         run(nxt[:2])
         lower(0, every)
-        run(nxt[2:4])
-        add_back(0, every)
-        weave(0, False)
-        run(nxt[4:])
-        banks0 = second_product(0)
+        z_tile(0)
+        add_turned(0, 0)
+        add_turned(0, P)
+        run(nxt[2:])
+        upper(1, lo)
+        upper(1, hi)
+        lower(1, lo)
+        lower(1, hi)
+        z_tile(1)
+        add_turned(1, 0)
+        second_product(0)
         nxt = gathers(2)
-        upper(1, every)
-        run(nxt[0:4:2])
-        lower(1, every)
-        run(nxt[4::2])
-        add_back(1, every)
-        weave(1, False)
-        for t in range(PACK):
-            h_window(0, banks0, t)
-        h_plain(0, banks0)
+        run(nxt[0::2])
         run(nxt[1::2])
-        banks1 = second_product(1)
-        alloc(2)
-        lo, hi = slice(0, 2), slice(2, 4)
         upper(2, lo)
         upper(2, hi)
         lower(2, lo)
+        second_product(1)
         lower(2, hi)
+        z32[2] = keep.tile([P, PACK, P], F32, name="z32", tag="z16_1", align_bytes=64)
         add_back(2, lo)
         add_back(2, hi)
-        weave(2, True)
-        banks2 = second_product(2)
-        h_window(1, banks1, 0)
-        h_window(2, banks2, 0)
-        h_plain(1, banks1)
-        h_plain(2, banks2)
-        for t in range(1, PACK):
-            h_window(1, banks1, t)
-            h_window(2, banks2, t)
+        z_tile(2)
+        weave(2, lo)
+        weave(2, hi)
+        second_product(2)
+        h_window(0)
+        h_plain(0, 2)
+        h_window(1)
+        h_plain(2, 4)
+        h_window(2)
+        h_window(3)
 
         out_rows = out_0.rearrange("(p t) c -> p t c", t=PACK)
         res = keep.tile([P, PACK, S], F32, name="res")
@@ -299,11 +317,17 @@ def tile_picked_laymedsendg_none_po_kernel(
         finish(3, halves[0])
         nc.scalar.copy(out=o16[0][:], in_=res[:, :, halves[0]].rearrange("p t c -> p c t"))
         finish(3, halves[1])
-        nc.vector.tensor_copy(out=o16[1][:], in_=res[:, :, halves[1]].rearrange("p t c -> p c t"))
-        for half in (1, 0):
-            cols = halves[half]
-            nc.vector.quantize_mx(out=ow[:, cols].bitcast(FP8X4), scales=osc[:, cols], in_=o16[half][:].rearrange("p c t -> p (c t)"))
-            nc.sync.dma_start(out=words_out[:, cols], in_=ow[:, cols].bitcast(I32))
+        for part in range(2):
+            nc.vector.tensor_copy(
+                out=o16[1][:, part * P : (part + 1) * P, :],
+                in_=res[:, :, HALF + part * P : HALF + (part + 1) * P].rearrange("p t c -> p c t"),
+            )
+        for part in range(2):
+            cols = slice(HALF + part * P, HALF + (part + 1) * P)
+            nc.vector.quantize_mx(out=ow[:, cols].bitcast(FP8X4), scales=osc[:, cols], in_=o16[1][:, part * P : (part + 1) * P, :].rearrange("p c t -> p (c t)"))
+        nc.sync.dma_start(out=words_out[:, halves[1]], in_=ow[:, halves[1]].bitcast(I32))
+        nc.vector.quantize_mx(out=ow[:, halves[0]].bitcast(FP8X4), scales=osc[:, halves[0]], in_=o16[0][:].rearrange("p c t -> p (c t)"))
+        nc.sync.dma_start(out=words_out[:, halves[0]], in_=ow[:, halves[0]].bitcast(I32))
         for q in range(4):
             queue = nc.scalar if q % 2 else nc.sync
             queue.dma_start(out=out_2[0, 4 * q : 4 * q + 4, :].bitcast(I32), in_=osc[32 * q : 32 * q + 4, :].bitcast(I32))

@@ -67,7 +67,8 @@ def tile_picked_laymedsendg_none_po_kernel(
         w1s_raw = keep.tile([P, S], U8, name="w1s_raw")
         xs_all = keep.tile([P, TOKENS], U8, name="xs_all")
         w2s_raw = keep.tile([P, S], U8, name="w2s_raw")
-        nc.gpsimd.memset(xs_all[:].bitcast(I32), 0)
+        nc.vector.memset(xs_all[:, : TOKENS // 2].bitcast(I32), 0)
+        nc.gpsimd.memset(xs_all[:, TOKENS // 2 :].bitcast(I32), 0)
         nc.vector.memset(w1s_raw[:].bitcast(I32), 0)
         nc.vector.memset(w2s_raw[:].bitcast(I32), 0)
 
@@ -77,13 +78,12 @@ def tile_picked_laymedsendg_none_po_kernel(
         gain = keep.tile([P, PACK], F32, name="gain")
 
         offs_t = load_list("offs_t", offs)
-        nc.sync.dma_start(out=w1w_raw[:].bitcast(I32), in_=w1_words[0].bitcast(I32))
-        nc.sync.dma_start(out=xw_all[:].bitcast(I32), in_=x_words[0].rearrange("p c r -> p (c r)").bitcast(I32))
-        load_scale_rows(nc.scalar, xs_all, x_scales, range(4))
-        load_scale_rows(nc.scalar, w1s_raw, w1_scales, range(3))
         nc.gpsimd.dma_start(out=gain[:], in_=gn.rearrange("(p t) o -> p (t o)", t=PACK))
-        load_scale_rows(nc.gpsimd, w1s_raw, w1_scales, range(3, 4))
-        nc.gpsimd.dma_start(out=w2w_raw[:].bitcast(I32), in_=w2_words[0].bitcast(I32))
+        nc.sync.dma_start(out=w1w_raw[:].bitcast(I32), in_=w1_words[0].bitcast(I32))
+        nc.sync.dma_start(out=w2w_raw[:].bitcast(I32), in_=w2_words[0].bitcast(I32))
+        load_scale_rows(nc.sync, xs_all, x_scales, range(4))
+        nc.sync.dma_start(out=xw_all[:].bitcast(I32), in_=x_words[0].rearrange("p c r -> p (c r)").bitcast(I32))
+        load_scale_rows(nc.sync, w1s_raw, w1_scales, range(4))
         n1_t = load_list("n1_t", n1)
         n2_t = load_list("n2_t", n2)
         load_scale_rows(nc.sync, w2s_raw, w2_scales, range(4))
@@ -93,7 +93,6 @@ def tile_picked_laymedsendg_none_po_kernel(
         make_identity(nc, ident[:])
 
         w1w = deal_words("w1w", w1w_raw, "w1w")
-        w1s = deal_scales("w1s", w1s_raw)
 
         xs = keep.tile([P, S], U8, name="xs", align_bytes=64)
         nc.vector.tensor_copy(xs[:], xs_all[:].indirect(offs_t[:]))
@@ -105,6 +104,8 @@ def tile_picked_laymedsendg_none_po_kernel(
         for half in range(2):
             xw.append(keep.tile([P, HALF], U32, name=f"xw{half}", align_bytes=64))
             nc.vector.tensor_copy(xw[half][:], xw_all[:].indirect(entries(offs_t, half * HALF, HALF)))
+            if half == 0:
+                w1s = deal_scales("w1s", w1s_raw)
         y_banks = [psum.tile([P, 2, HALF], F32, name=f"y_ps{b}", tag=f"shared{b}") for b in range(4)]
 
         def first_product(half, t):
@@ -131,7 +132,7 @@ def tile_picked_laymedsendg_none_po_kernel(
         for t in range(PACK):
             y_out(y_own[:, t, HALF:], 1, t)
 
-        w2w = deal_words("w2w", w2w_raw, "xw_all")
+        w2w = deal_words("w2w", w2w_raw, "w2w")
         w2s = deal_scales("w2s", w2s_raw)
 
         h_win = [keep.tile([P, S], F32, name=f"h_win{t}") for t in range(PACK)]
@@ -143,7 +144,7 @@ def tile_picked_laymedsendg_none_po_kernel(
         def gathers(c):
             start, n = CHUNKS[c]
             da[c] = keep.tile([P, PACK, n], F32, name=f"da{c}")
-            db[c] = keep.tile([P, PACK, n], F32, name=f"db{c}", tag="z16_0" if c == 2 else f"db{c}", align_bytes=64)
+            db[c] = keep.tile([P, PACK, n], F32, name=f"db{c}", align_bytes=64)
             steps = []
             for t in range(PACK):
                 for dst, lst in ((da[c], n1_t), (db[c], n2_t)):
@@ -162,11 +163,12 @@ def tile_picked_laymedsendg_none_po_kernel(
 
         def add_back(c, cols):
             start = CHUNKS[c][0]
-            nc.vector.tensor_tensor(z32[c][:, :, cols], med[c][:, :, cols], y_own[:, :, start + cols.start : start + cols.stop], ALU.add)
+            own = y_own[:, :, start + cols.start : start + cols.stop]
+            nc.vector.tensor_tensor(z16[c][:, cols, :], med[c][:, :, cols].rearrange("p t c -> p c t"), own.rearrange("p t c -> p c t"), ALU.add)
 
         def alloc(c):
             n = CHUNKS[c][1]
-            mid[c] = keep.tile([P, PACK, n], F32, name=f"mid{c}", align_bytes=64)
+            mid[c] = keep.tile([P, PACK, n], F32, name=f"mid{c}", tag="z16_0" if c == 2 else f"mid{c}", align_bytes=64)
             med[c] = keep.tile([P, PACK, n], F32, name=f"med{c}")
 
         z16 = {}
@@ -174,18 +176,24 @@ def tile_picked_laymedsendg_none_po_kernel(
         h_banks = [[], [], []]
 
         def z_tile(c):
-            z16[c] = keep.tile([P, CHUNKS[c][1], PACK], BF16, name=f"z16{c}", tag=f"z16_{c}", align_bytes=64)
+            z16[c] = keep.tile([P, CHUNKS[c][1], PACK], BF16, name=f"z16{c}", tag=f"z16_{min(c, 1)}", align_bytes=64)
 
         def weave(c, cols):
             nc.vector.tensor_copy(out=z16[c][:, cols, :], in_=z32[c][:, :, cols].rearrange("p t c -> p c t"))
 
-        def add_turned(c, off):
-            start = CHUNKS[c][0] + off
-            blk = start // P
-            turned = psum.tile([P, PACK, P], F32, name=f"turned{blk}", tag=f"shared{blk % 2}")
+        turned_banks = {}
+
+        def open_turned(blk):
+            turned = psum.tile([P, PACK, P], F32, name=f"turned{blk}", tag=("shared0", "shared1", "h3")[blk])
+            turned_banks[blk] = turned
             for t in range(PACK):
-                nc.tensor.matmul(turned[:, t, :], lhsT=y_own[:, t, start : start + P], rhs=ident[:], start=True, stop=False, is_transpose=True)
-                nc.tensor.matmul(turned[:, t, :], lhsT=med[c][:, t, off : off + P], rhs=ident[:], start=False, stop=True, is_transpose=True)
+                nc.tensor.matmul(turned[:, t, :], lhsT=y_own[:, t, blk * P : (blk + 1) * P], rhs=ident[:], start=(t == 0), stop=False, is_transpose=True)
+
+        def add_turned(c, off):
+            blk = (CHUNKS[c][0] + off) // P
+            turned = turned_banks[blk]
+            for t in range(PACK):
+                nc.tensor.matmul(turned[:, t, :], lhsT=med[c][:, t, off : off + P], rhs=ident[:], start=False, stop=(t == PACK - 1), is_transpose=True)
             pairs = keep.tile([P, 2, P, 2], BF16, name=f"pairs{blk}")
             nc.scalar.copy(out=pairs[:], in_=turned[:].rearrange("j (u e) p -> j u p e", e=2))
             words = pairs[:].rearrange("j u p e -> j (u p e)").bitcast(F32)
@@ -231,8 +239,10 @@ def tile_picked_laymedsendg_none_po_kernel(
             nc.scalar.activation(out=gate[:, t, :], in_=h_own[:, t, :], func=ACT.Sigmoid)
 
         every, lo, hi = slice(0, HALF), slice(0, P // 2), slice(P // 2, P)
-        for c in range(3):
-            alloc(c)
+        alloc(0)
+        alloc(1)
+        for blk in range(3):
+            open_turned(blk)
         run(gathers(0))
         nxt = gathers(1)
         upper(0, every)
@@ -248,21 +258,17 @@ def tile_picked_laymedsendg_none_po_kernel(
         lower(1, hi)
         z_tile(1)
         add_turned(1, 0)
+        run(gathers(2))
         second_product(0)
-        nxt = gathers(2)
-        run(nxt[0::2])
-        run(nxt[1::2])
+        alloc(2)
         upper(2, lo)
         upper(2, hi)
         lower(2, lo)
         second_product(1)
         lower(2, hi)
-        z32[2] = keep.tile([P, PACK, P], F32, name="z32", tag="z16_1", align_bytes=64)
+        z_tile(2)
         add_back(2, lo)
         add_back(2, hi)
-        z_tile(2)
-        weave(2, lo)
-        weave(2, hi)
         second_product(2)
         h_window(0)
         h_plain(0, 2)

@@ -137,7 +137,7 @@ def tile_picked_laymedsendg_none_po_kernel(
 
         h_win = [keep.tile([P, S], F32, name=f"h_win{t}") for t in range(PACK)]
         h_own = keep.tile([P, PACK, S], F32, name="h_own")
-        gate = keep.tile([P, PACK, S], F32, name="gate")
+        gate = {}
 
         da, db, mid, med, z32 = {}, {}, {}, {}, {}
 
@@ -236,7 +236,8 @@ def tile_picked_laymedsendg_none_po_kernel(
                         nc.scalar.copy(out=h_own[:, lo_t:hi_t, start : start + n], in_=bank[:, lo_t - b_first : hi_t - b_first, :])
 
         def gates(t):
-            nc.scalar.activation(out=gate[:, t, :], in_=h_own[:, t, :], func=ACT.Sigmoid)
+            gate[t] = keep.tile([P, S], F32, name=f"gate{t}", tag=f"held{t + 1}")
+            nc.scalar.activation(out=gate[t][:], in_=h_own[:, t, :], func=ACT.Sigmoid)
 
         every, lo, hi = slice(0, HALF), slice(0, P // 2), slice(P // 2, P)
         alloc(0)
@@ -280,49 +281,68 @@ def tile_picked_laymedsendg_none_po_kernel(
         out_rows = out_0.rearrange("(p t) c -> p t c", t=PACK)
         res = keep.tile([P, PACK, S], F32, name="res")
         rise = {}
+        diffs = {}
         sent = {}
 
         def look_up(t):
-            diff = keep.tile([P, S], F32, name=f"diff{t}")
+            diff = keep.tile([P, S], F32, name=f"diff{t}", tag=f"diff{t}")
             for half in range(2):
                 cols = slice(half * HALF, (half + 1) * HALF)
                 nc.vector.tensor_tensor(diff[:, cols], h_win[t][:].indirect(entries(n4_t, half * HALF, HALF)), h_own[:, t, cols], ALU.subtract)
-            rise[t] = keep.tile([P, S], F32, name=f"rise{t}")
-            nc.scalar.activation(out=rise[t][:], in_=diff[:], func=ACT.Relu)
+            diffs[t] = diff
+
+        def rises(t):
+            rise[t] = keep.tile([P, S], F32, name=f"rise{t}", tag=f"rise{min(t, 1)}")
+            nc.scalar.activation(out=rise[t][:], in_=diffs[t][:], func=ACT.Relu)
 
         def send(t):
             sent[t] = keep.tile([P, 2 * S], F32, name=f"sent{t}")
             nc.vector.tensor_tensor(sent[t][:].indirect(n3_t[:]), h_own[:, t, :], rise[t][:], ALU.add)
 
-        def finish(t, cols):
-            nc.vector.tensor_tensor(res[:, t, cols], sent[t][:, cols], gate[:, t, cols], ALU.mult)
+        def larger(t):
+            turned = psum.tile([P, PACK, P], F32, name=f"sm_turned{t}", tag=f"h{t - 1}")
+            for part, src in enumerate((h_own[:, t, :], rise[t][:])):
+                for b in range(PACK):
+                    nc.tensor.matmul(turned[:, b, :], lhsT=src[:, b * P : (b + 1) * P], rhs=ident[:], start=(part == 0 and b == 0), stop=(part == 1 and b == PACK - 1), is_transpose=True)
+            held = keep.tile([P, PACK, P], F32, name=f"sm_held{t}", tag=f"held{t}")
+            nc.scalar.copy(out=held[:], in_=turned[:])
+            back = psum.tile([P, PACK, P], F32, name=f"sm_back{t}", tag=("shared0", "shared2", "shared3")[t - 1])
+            for b in range(PACK):
+                nc.tensor.transpose(back[:, b, :], held[:, b, :], ident[:])
+            sm[t] = keep.tile([P, S], F32, name=f"sm{t}")
+            nc.scalar.copy(out=sm[t][:], in_=back[:].rearrange("p b j -> p (b j)"))
+
+        def send_copy(t):
+            sent[t] = keep.tile([P, 2 * S], F32, name=f"sent{t}")
+            nc.vector.tensor_copy(sent[t][:].indirect(n3_t[:]), sm[t][:])
+
+        def finish(engine, t, cols):
+            engine.tensor_tensor(res[:, t, cols], sent[t][:, cols], gate[t][:, cols], ALU.mult)
             nc.sync.dma_start(out=out_rows[:, t, cols], in_=res[:, t, cols])
 
         whole = slice(0, S)
-        look_up(0)
-        look_up(1)
-        gates(0)
+        sm = {}
+        for t in range(PACK):
+            look_up(t)
+        rises(0)
         send(0)
-        look_up(2)
-        gates(1)
-        send(1)
-        finish(0, whole)
-        look_up(3)
-        gates(2)
-        gates(3)
-        send(2)
-        finish(1, whole)
-        finish(2, whole)
-        send(3)
+        for t in range(1, PACK):
+            rises(t)
+            larger(t)
+            send_copy(t)
+        for t in range(PACK - 1):
+            gates(t)
+            finish(nc.gpsimd, t, whole)
+        gates(PACK - 1)
 
         ow = keep.tile([P, S], U32, name="ow", align_bytes=64)
         osc = keep.tile([P, S], U8, name="osc", align_bytes=64)
         words_out = out_1[0].rearrange("p c r -> p (c r)").bitcast(I32)
         o16 = [keep.tile([P, HALF, PACK], BF16, name=f"o16{half}", align_bytes=64) for half in range(2)]
         halves = [slice(half * HALF, (half + 1) * HALF) for half in range(2)]
-        finish(3, halves[0])
+        finish(nc.vector, 3, halves[0])
         nc.scalar.copy(out=o16[0][:], in_=res[:, :, halves[0]].rearrange("p t c -> p c t"))
-        finish(3, halves[1])
+        finish(nc.vector, 3, halves[1])
         for part in range(2):
             nc.vector.tensor_copy(
                 out=o16[1][:, part * P : (part + 1) * P, :],

from contextlib import ExitStack

import concourse.mybir as mybir
from concourse.masks import make_identity

F32 = mybir.dt.float32
BF16 = mybir.dt.bfloat16
I32 = mybir.dt.int32
U32 = mybir.dt.uint32
U16 = mybir.dt.uint16
U8 = mybir.dt.uint8
FP8X4 = mybir.dt.float8_e4m3fn_x4
FP4X4 = mybir.dt.float4_e2m1fn_x4
ALU = mybir.AluOpType
ACT = mybir.ActivationFunctionType

P = 128
PACK = 4
TOKENS = 2048
S = 512
HALF = S // 2
CHUNKS = ((0, 256), (256, 128), (384, 128))
H_BANKS = (
    ((0, 2, "h0"), (2, 4, "h1")),
    ((0, 4, "h2"),),
    ((0, 1, "h3"), (1, 4, "shared1")),
)
FLOPS = 2 * 2 * 512 * 512 * 512


def tile_picked_laymedsendg_none_po_kernel(
    tc, x_words, x_scales, w1_words, w1_scales, gn, w2_words, w2_scales, offs, n1, n2, n3, n4, out_0, out_1, out_2
):
    nc = tc.nc
    with ExitStack() as ctx:
        keep = ctx.enter_context(tc.tile_pool(name="keep", bufs=1))
        psum = ctx.enter_context(tc.psum_pool(name="psum", bufs=1))

        def load_scale_rows(queue, tile, rows, quadrants):
            for q in quadrants:
                queue.dma_start(out=tile[32 * q : 32 * q + 4, :].bitcast(I32), in_=rows[0, 4 * q : 4 * q + 4, :].bitcast(I32))

        def load_list(name, src):
            tile = keep.tile([P, S // 16], U16, name=name)
            nc.sync.dma_start(tile[:], src)
            return tile

        def entries(lst, start, count):
            return lst[:, start // 16 : (start + count) // 16]

        def deal_words(name, raw, tag):
            dealt = keep.tile([P, 2 * S], U8, name=name, tag=tag, align_bytes=64)
            nc.vector.tensor_copy(
                out=dealt[:].rearrange("p (t m e) -> p t m e", t=PACK, e=2),
                in_=raw[:].rearrange("p (m t e) -> p t m e", t=PACK, e=2),
            )
            return dealt

        def deal_scales(name, raw):
            dealt = keep.tile([P, S], U8, name=name, align_bytes=64)
            nc.vector.tensor_copy(
                out=dealt[:].rearrange("p (t m) -> p t m", t=PACK),
                in_=raw[:].rearrange("p (m t) -> p t m", t=PACK),
            )
            return dealt

        w1s_raw = keep.tile([P, S], U8, name="w1s_raw")
        xs_all = keep.tile([P, TOKENS], U8, name="xs_all")
        w2s_raw = keep.tile([P, S], U8, name="w2s_raw")
        nc.vector.memset(xs_all[:, : TOKENS // 2].bitcast(I32), 0)
        nc.gpsimd.memset(xs_all[:, TOKENS // 2 :].bitcast(I32), 0)
        nc.vector.memset(w1s_raw[:].bitcast(I32), 0)
        nc.vector.memset(w2s_raw[:].bitcast(I32), 0)

        w1w_raw = keep.tile([P, 2 * S], U8, name="w1w_raw")
        w2w_raw = keep.tile([P, 2 * S], U8, name="w2w_raw")
        xw_all = keep.tile([P, TOKENS], U32, name="xw_all", tag="xw_all", align_bytes=64)
        gain = keep.tile([P, PACK], F32, name="gain")

        offs_t = load_list("offs_t", offs)
        nc.gpsimd.dma_start(out=gain[:], in_=gn.rearrange("(p t) o -> p (t o)", t=PACK))
        nc.sync.dma_start(out=w1w_raw[:].bitcast(I32), in_=w1_words[0].bitcast(I32))
        nc.sync.dma_start(out=w2w_raw[:].bitcast(I32), in_=w2_words[0].bitcast(I32))
        load_scale_rows(nc.sync, xs_all, x_scales, range(4))
        nc.sync.dma_start(out=xw_all[:].bitcast(I32), in_=x_words[0].rearrange("p c r -> p (c r)").bitcast(I32))
        load_scale_rows(nc.sync, w1s_raw, w1_scales, range(4))
        n1_t = load_list("n1_t", n1)
        n2_t = load_list("n2_t", n2)
        load_scale_rows(nc.sync, w2s_raw, w2_scales, range(4))
        n4_t = load_list("n4_t", n4)
        n3_t = load_list("n3_t", n3)
        ident = keep.tile([P, P], F32, name="ident")
        make_identity(nc, ident[:])

        w1w = deal_words("w1w", w1w_raw, "w1w")

        xs = keep.tile([P, S], U8, name="xs", align_bytes=64)
        nc.vector.tensor_copy(xs[:], xs_all[:].indirect(offs_t[:]))

        y_win = [keep.tile([P, S], F32, name=f"y_win{t}") for t in range(PACK)]
        y_own = keep.tile([P, PACK, S], F32, name="y_own")
        y_ps = {}
        xw = []
        for half in range(2):
            xw.append(keep.tile([P, HALF], U32, name=f"xw{half}", align_bytes=64))
            nc.vector.tensor_copy(xw[half][:], xw_all[:].indirect(entries(offs_t, half * HALF, HALF)))
            if half == 0:
                w1s = deal_scales("w1s", w1s_raw)
        y_banks = [psum.tile([P, 2, HALF], F32, name=f"y_ps{b}", tag=f"shared{b}") for b in range(4)]

        def first_product(half, t):
            y_ps[half, t] = y_banks[2 * (t % 2) + half][:, t // 2, :]
            nc.tensor.matmul_mx(
                out=y_ps[half, t],
                lhsT=w1w[:, 2 * P * t : 2 * P * (t + 1)].bitcast(FP4X4),
                lhsT_scale=w1s[:, P * t : P * (t + 1)],
                rhs=xw[half][:].bitcast(FP8X4),
                rhs_scale=xs[:, half * HALF : (half + 1) * HALF],
                start=True,
                stop=True,
            )

        def y_out(dst, half, t):
            nc.scalar.activation(out=dst, in_=y_ps[half, t], func=ACT.Copy, scale=gain[:, t : t + 1])

        for t in range(PACK):
            first_product(0, t)
            first_product(1, t)
            y_out(y_win[t][:, :HALF], 0, t)
            y_out(y_own[:, t, :HALF], 0, t)
            y_out(y_win[t][:, HALF:], 1, t)
        for t in range(PACK):
            y_out(y_own[:, t, HALF:], 1, t)

        w2w = deal_words("w2w", w2w_raw, "w2w")
        w2s = deal_scales("w2s", w2s_raw)

        h_win = [keep.tile([P, S], F32, name=f"h_win{t}") for t in range(PACK)]
        h_own = keep.tile([P, PACK, S], F32, name="h_own")
        gate = {}

        da, db, mid, med, z32 = {}, {}, {}, {}, {}

        def gathers(c):
            start, n = CHUNKS[c]
            da[c] = keep.tile([P, PACK, n], F32, name=f"da{c}")
            db[c] = keep.tile([P, PACK, n], F32, name=f"db{c}", align_bytes=64)
            steps = []
            for t in range(PACK):
                for dst, lst in ((da[c], n1_t), (db[c], n2_t)):
                    steps.append((dst[:, t, :], y_win[t][:].indirect(entries(lst, start, n)), y_own[:, t, start : start + n]))
            return steps

        def run(steps):
            for dst, looked, own in steps:
                nc.vector.tensor_tensor(dst, looked, own, ALU.subtract)

        def upper(c, cols):
            nc.vector.scalar_tensor_tensor(out=mid[c][:, :, cols], in0=da[c][:, :, cols], scalar=0.0, in1=db[c][:, :, cols], op0=ALU.max, op1=ALU.min)

        def lower(c, cols):
            nc.vector.scalar_tensor_tensor(out=med[c][:, :, cols], in0=da[c][:, :, cols], scalar=0.0, in1=mid[c][:, :, cols], op0=ALU.min, op1=ALU.max)

        def add_back(c, cols):
            start = CHUNKS[c][0]
            own = y_own[:, :, start + cols.start : start + cols.stop]
            nc.vector.tensor_tensor(z16[c][:, cols, :], med[c][:, :, cols].rearrange("p t c -> p c t"), own.rearrange("p t c -> p c t"), ALU.add)

        def alloc(c):
            n = CHUNKS[c][1]
            mid[c] = keep.tile([P, PACK, n], F32, name=f"mid{c}", tag="z16_0" if c == 2 else f"mid{c}", align_bytes=64)
            med[c] = keep.tile([P, PACK, n], F32, name=f"med{c}")

        z16 = {}
        h_ps = {}
        h_banks = [[], [], []]

        def z_tile(c):
            z16[c] = keep.tile([P, CHUNKS[c][1], PACK], BF16, name=f"z16{c}", tag=f"z16_{min(c, 1)}", align_bytes=64)

        def weave(c, cols):
            nc.vector.tensor_copy(out=z16[c][:, cols, :], in_=z32[c][:, :, cols].rearrange("p t c -> p c t"))

        turned_banks = {}

        def open_turned(blk):
            turned = psum.tile([P, PACK, P], F32, name=f"turned{blk}", tag=("shared0", "shared1", "h3")[blk])
            turned_banks[blk] = turned
            for t in range(PACK):
                nc.tensor.matmul(turned[:, t, :], lhsT=y_own[:, t, blk * P : (blk + 1) * P], rhs=ident[:], start=(t == 0), stop=False, is_transpose=True)

        def add_turned(c, off):
            blk = (CHUNKS[c][0] + off) // P
            turned = turned_banks[blk]
            for t in range(PACK):
                nc.tensor.matmul(turned[:, t, :], lhsT=med[c][:, t, off : off + P], rhs=ident[:], start=False, stop=(t == PACK - 1), is_transpose=True)
            pairs = keep.tile([P, 2, P, 2], BF16, name=f"pairs{blk}")
            nc.scalar.copy(out=pairs[:], in_=turned[:].rearrange("j (u e) p -> j u p e", e=2))
            words = pairs[:].rearrange("j u p e -> j (u p e)").bitcast(F32)
            back = psum.tile([P, 2, P], F32, name=f"back{blk}", tag=f"shared{2 + blk % 2}")
            for u in range(2):
                nc.tensor.transpose(back[:, u, :], words[:, u * P : (u + 1) * P], ident[:])
            dst = z16[c][:, off : off + P, :].rearrange("p c t -> p (c t)").bitcast(F32)
            nc.scalar.copy(out=dst.rearrange("p (j u) -> p j u", u=2), in_=back[:].rearrange("p u j -> p j u"))

        def second_product(c):
            start, n = CHUNKS[c]
            cols = slice(start, start + n)
            zw = keep.tile([P, n], U32, name=f"zw{c}", align_bytes=64)
            zs = keep.tile([P, n], U8, name=f"zs{c}", align_bytes=64)
            nc.vector.quantize_mx(out=zw[:].bitcast(FP8X4), scales=zs[:], in_=z16[c][:].rearrange("p c t -> p (c t)"))
            for first, last, tag in H_BANKS[c]:
                bank = psum.tile([P, last - first, n], F32, name=f"h_ps{c}{first}", tag=tag)
                h_banks[c].append((first, last, bank))
                for t in range(first, last):
                    h_ps[c, t] = bank[:, t - first, :]
                    nc.tensor.matmul_mx(
                        out=h_ps[c, t],
                        lhsT=w2w[:, 2 * P * t : 2 * P * (t + 1)].bitcast(FP4X4),
                        lhsT_scale=w2s[:, P * t : P * (t + 1)],
                        rhs=zw[:].bitcast(FP8X4),
                        rhs_scale=zs[:],
                        start=True,
                        stop=True,
                    )

        def h_window(t):
            for c, (start, n) in enumerate(CHUNKS):
                nc.scalar.copy(out=h_win[t][:, start : start + n], in_=h_ps[c, t])

        def h_plain(first, last):
            for c, (start, n) in enumerate(CHUNKS):
                for b_first, b_last, bank in h_banks[c]:
                    lo_t, hi_t = max(first, b_first), min(last, b_last)
                    if lo_t < hi_t:
                        nc.scalar.copy(out=h_own[:, lo_t:hi_t, start : start + n], in_=bank[:, lo_t - b_first : hi_t - b_first, :])

        def gates(t):
            gate[t] = keep.tile([P, S], F32, name=f"gate{t}", tag=f"held{t + 1}")
            nc.scalar.activation(out=gate[t][:], in_=h_own[:, t, :], func=ACT.Sigmoid)

        every, lo, hi = slice(0, HALF), slice(0, P // 2), slice(P // 2, P)
        alloc(0)
        alloc(1)
        for blk in range(3):
            open_turned(blk)
        run(gathers(0))
        nxt = gathers(1)
        upper(0, every)
        run(nxt[:2])
        lower(0, every)
        z_tile(0)
        add_turned(0, 0)
        add_turned(0, P)
        run(nxt[2:])
        upper(1, lo)
        upper(1, hi)
        lower(1, lo)
        lower(1, hi)
        z_tile(1)
        add_turned(1, 0)
        run(gathers(2))
        second_product(0)
        alloc(2)
        upper(2, lo)
        upper(2, hi)
        lower(2, lo)
        second_product(1)
        lower(2, hi)
        z_tile(2)
        add_back(2, lo)
        add_back(2, hi)
        second_product(2)
        h_window(0)
        h_plain(0, 2)
        h_window(1)
        h_plain(2, 4)
        h_window(2)
        h_window(3)

        out_rows = out_0.rearrange("(p t) c -> p t c", t=PACK)
        res = keep.tile([P, PACK, S], F32, name="res")
        rise = {}
        diffs = {}
        sent = {}

        def look_up(t):
            diff = keep.tile([P, S], F32, name=f"diff{t}", tag=f"diff{t}")
            for half in range(2):
                cols = slice(half * HALF, (half + 1) * HALF)
                nc.vector.tensor_tensor(diff[:, cols], h_win[t][:].indirect(entries(n4_t, half * HALF, HALF)), h_own[:, t, cols], ALU.subtract)
            diffs[t] = diff

        def rises(t):
            rise[t] = keep.tile([P, S], F32, name=f"rise{t}", tag=f"rise{min(t, 1)}")
            nc.scalar.activation(out=rise[t][:], in_=diffs[t][:], func=ACT.Relu)

        def send(t):
            sent[t] = keep.tile([P, 2 * S], F32, name=f"sent{t}")
            nc.vector.tensor_tensor(sent[t][:].indirect(n3_t[:]), h_own[:, t, :], rise[t][:], ALU.add)

        def larger(t):
            turned = psum.tile([P, PACK, P], F32, name=f"sm_turned{t}", tag=f"h{t - 1}")
            for part, src in enumerate((h_own[:, t, :], rise[t][:])):
                for b in range(PACK):
                    nc.tensor.matmul(turned[:, b, :], lhsT=src[:, b * P : (b + 1) * P], rhs=ident[:], start=(part == 0 and b == 0), stop=(part == 1 and b == PACK - 1), is_transpose=True)
            held = keep.tile([P, PACK, P], F32, name=f"sm_held{t}", tag=f"held{t}")
            nc.scalar.copy(out=held[:], in_=turned[:])
            back = psum.tile([P, PACK, P], F32, name=f"sm_back{t}", tag=("shared0", "shared2", "shared3")[t - 1])
            for b in range(PACK):
                nc.tensor.transpose(back[:, b, :], held[:, b, :], ident[:])
            sm[t] = keep.tile([P, S], F32, name=f"sm{t}")
            nc.scalar.copy(out=sm[t][:], in_=back[:].rearrange("p b j -> p (b j)"))

        def send_copy(t):
            sent[t] = keep.tile([P, 2 * S], F32, name=f"sent{t}")
            nc.vector.tensor_copy(sent[t][:].indirect(n3_t[:]), sm[t][:])

        def finish(engine, t, cols):
            engine.tensor_tensor(res[:, t, cols], sent[t][:, cols], gate[t][:, cols], ALU.mult)
            nc.sync.dma_start(out=out_rows[:, t, cols], in_=res[:, t, cols])

        whole = slice(0, S)
        sm = {}
        for t in range(PACK):
            look_up(t)
        rises(0)
        send(0)
        for t in range(1, PACK):
            rises(t)
            larger(t)
            send_copy(t)
        for t in range(PACK - 1):
            gates(t)
            finish(nc.gpsimd, t, whole)
        gates(PACK - 1)

        ow = keep.tile([P, S], U32, name="ow", align_bytes=64)
        osc = keep.tile([P, S], U8, name="osc", align_bytes=64)
        words_out = out_1[0].rearrange("p c r -> p (c r)").bitcast(I32)
        o16 = [keep.tile([P, HALF, PACK], BF16, name=f"o16{half}", align_bytes=64) for half in range(2)]
        halves = [slice(half * HALF, (half + 1) * HALF) for half in range(2)]
        finish(nc.vector, 3, halves[0])
        nc.scalar.copy(out=o16[0][:], in_=res[:, :, halves[0]].rearrange("p t c -> p c t"))
        finish(nc.vector, 3, halves[1])
        for part in range(2):
            nc.vector.tensor_copy(
                out=o16[1][:, part * P : (part + 1) * P, :],
                in_=res[:, :, HALF + part * P : HALF + (part + 1) * P].rearrange("p t c -> p c t"),
            )
        for part in range(2):
            cols = slice(HALF + part * P, HALF + (part + 1) * P)
            nc.vector.quantize_mx(out=ow[:, cols].bitcast(FP8X4), scales=osc[:, cols], in_=o16[1][:, part * P : (part + 1) * P, :].rearrange("p c t -> p (c t)"))
        nc.sync.dma_start(out=words_out[:, halves[1]], in_=ow[:, halves[1]].bitcast(I32))
        nc.vector.quantize_mx(out=ow[:, halves[0]].bitcast(FP8X4), scales=osc[:, halves[0]], in_=o16[0][:].rearrange("p c t -> p (c t)"))
        nc.sync.dma_start(out=words_out[:, halves[0]], in_=ow[:, halves[0]].bitcast(I32))
        for q in range(4):
            queue = nc.scalar if q % 2 else nc.sync
            queue.dma_start(out=out_2[0, 4 * q : 4 * q + 4, :].bitcast(I32), in_=osc[32 * q : 32 * q + 4, :].bitcast(I32))
